import numpy as np
import ml_dtypes


def mxq(x, axis, fmt="e4m3"):
    dtype, down = {"e4m3": (ml_dtypes.float8_e4m3fn, 7), "e5m2": (ml_dtypes.float8_e5m2, 14)}[fmt]
    v = np.moveaxis(np.asarray(x, np.float32).astype(ml_dtypes.bfloat16).astype(np.float64), axis, -1)
    blocks = v.reshape(v.shape[:-1] + (-1, 32))
    amax = np.abs(blocks).max(-1, keepdims=True)
    byte = np.maximum(np.where(amax > 0, np.frexp(amax)[1] - 1 + 127, 0) - down, 1)
    scale = np.exp2(byte - 127.0)
    codes = (blocks / scale).astype(np.float32).astype(dtype).astype(np.float64)
    return np.moveaxis((codes * scale).reshape(v.shape), -1, axis)


WIDE = False


def mx_kscale(k):
    if not WIDE:
        return np.ones(k)
    levels = np.array([10, -10, 5, -5, 0])
    if k % 512:
        return np.exp2(np.random.permutation(np.resize(levels, k // 32))).repeat(32)
    a = np.empty((k // 512, 16))
    for p in range(k // 512):
        a[p, :8] = np.random.permutation(np.resize(levels, 8))
        for g in range(8):
            far = levels[np.abs(levels - a[p, g]) >= 10]
            a[p, g + 8] = far[np.random.randint(len(far))]
    return np.exp2(a.ravel()).repeat(32)


BF16 = ml_dtypes.bfloat16


def bf(x):
    return np.asarray(x, np.float32).astype(BF16)


def f64(x):
    return np.asarray(x).astype(np.float64)


E2M1 = np.array([0.0, 0.5, 1.0, 1.5, 2.0, 3.0, 4.0, 6.0, -0.0, -0.5, -1.0, -1.5, -2.0, -3.0, -4.0, -6.0])


def pack_weight(w, fmt):
    k, n = w.shape
    w = f64(bf(w)).reshape(k // 32, 32, n)
    amax = np.abs(w).max(1)
    if fmt == "e4m3":
        byte = np.frexp(amax)[1] - 1 + 127 - 7
    else:
        mant, ex = np.frexp(amax / 6.0)
        byte = np.where(mant > 0.5, ex, ex - 1) + 127
    byte = np.clip(np.where(amax > 0, byte, 1), 1, 254)
    scaled = (w * np.exp2(127.0 - byte)[:, None, :]).reshape(k, n).astype(np.float32)
    by_word = np.ascontiguousarray(scaled.reshape(k // 512, 128, 4, n).transpose(0, 1, 3, 2))
    if fmt == "e4m3":
        words = by_word.astype(ml_dtypes.float8_e4m3fn).view(np.uint8)
    else:
        c = by_word.astype(ml_dtypes.float4_e2m1fn).view(np.uint8) & 0xF
        words = c[..., 0::2] | (c[..., 1::2] << 4)
    return np.ascontiguousarray(words), np.ascontiguousarray(byte.astype(np.uint8).reshape(k // 512, 16, n))


def unpack_weight(words, scales, fmt):
    g, p, n, _ = words.shape
    if fmt == "e4m3":
        vals = np.ascontiguousarray(words).view(ml_dtypes.float8_e4m3fn).astype(np.float64)
    else:
        nib = np.empty((g, p, n, 4), np.uint8)
        nib[..., 0::2] = words & 0xF
        nib[..., 1::2] = words >> 4
        vals = E2M1[nib]
    vals = vals * np.repeat(np.exp2(scales.astype(np.float64) - 127.0), 8, axis=1)[..., None]
    return vals.transpose(0, 1, 3, 2).reshape(g * 512, n)
def pack4(w):
    words, scales = pack_weight(w, "e2m1")
    return words.reshape(words.shape[0], 128, -1), scales


def unpack4(words, scales):
    return unpack_weight(words.reshape(words.shape[0], 128, -1, 2), scales, "e2m1")


T, C, F, S, N = 2048, 1024, 512, 1024, 1024


def setup_inputs():
    a, r = mx_kscale(C), mx_kscale(F)
    t = mx_kscale(S)
    time = np.random.uniform(0.5, 1.5, T)
    knots = np.random.uniform(0.0, 1.0, C)
    hinge = np.maximum(time[None, :] - knots[:, None], 0.0)
    angle = 2 * np.pi * np.arange(1, F // 2 + 1)[:, None] * time[None, :]
    fourier = np.concatenate([np.sin(angle), np.cos(angle)], axis=0)
    slopes = np.random.standard_normal((C, S)) / np.sqrt(C)
    beta = np.random.standard_normal((F, S)) / np.sqrt(F)
    mix = np.random.standard_normal((S, N)) / np.sqrt(S)
    hinge_words, hinge_scales = pack4(hinge * a[:, None])
    slopes_words, slopes_scales = pack4(slopes / a[:, None] * t)
    fourier_words, fourier_scales = pack4(fourier * r[:, None])
    beta_words, beta_scales = pack4(beta / r[:, None])
    mix_words, mix_scales = pack_weight(mix / t[:, None], "e4m3")
    return {"hinge_words": hinge_words, "hinge_scales": hinge_scales,
            "slopes_words": slopes_words, "slopes_scales": slopes_scales,
            "fourier_words": fourier_words, "fourier_scales": fourier_scales,
            "beta_words": beta_words, "beta_scales": beta_scales,
            "mix_words": mix_words, "mix_scales": mix_scales,
            "level": bf(0.3 * np.random.standard_normal(N))}


def reference(hinge_words, hinge_scales, slopes_words, slopes_scales, fourier_words, fourier_scales,
              beta_words, beta_scales, mix_words, mix_scales, level):
    trend = unpack4(hinge_words, hinge_scales).T @ unpack4(slopes_words, slopes_scales)
    season = unpack4(fourier_words, fourier_scales).T @ unpack4(beta_words, beta_scales)
    y = trend * (1.0 + season)
    return (mxq(y, 1, "e4m3") @ unpack_weight(mix_words, mix_scales, "e4m3")) + f64(level)

@@ -1,0 +1,245 @@
+from contextlib import ExitStack
+
+import concourse.mybir as mybir
+
+T, C, F, S, N = 2048, 1024, 512, 1024, 1024
+FLOPS = 2 * T * S * (C + F) + 2 * T * S * N
+
+F32 = mybir.dt.float32
+BF16 = mybir.dt.bfloat16
+I32 = mybir.dt.int32
+U32 = mybir.dt.uint32
+U8 = mybir.dt.uint8
+FP4X4 = mybir.dt.float4_e2m1fn_x4
+FP8X4 = mybir.dt.float8_e4m3fn_x4
+ADD = mybir.AluOpType.add
+MULT = mybir.AluOpType.mult
+IDENTITY = mybir.ActivationFunctionType.Identity
+
+P = 128
+PACK = 4
+K_PASS = P * PACK
+T_CHUNK = 512
+T_TILE = 128
+CHUNKS = T // T_CHUNK
+TILES = T_CHUNK // T_TILE
+GROUPS = S // K_PASS
+LAG = 2
+
+
+def tile_prophet_trend_seasonality_s4_kernel(
+    tc, hinge_words, hinge_scales, slopes_words, slopes_scales, fourier_words, fourier_scales,
+    beta_words, beta_scales, mix_words, mix_scales, level, out,
+):
+    nc = tc.nc
+    with ExitStack() as ctx:
+        ctx.enter_context(tc.manual_schedule())
+        keep = ctx.enter_context(tc.tile_pool(name="keep", bufs=1))
+        work = ctx.enter_context(tc.tile_pool(name="work", bufs=4))
+        psum = ctx.enter_context(tc.psum_pool(name="psum", bufs=2))
+
+        def byte_tile(label, shape):
+            return keep.tile(shape, U8, name=label, align_bytes=64)
+
+        beta_raw = byte_tile("beta_raw", [P, 2 * S])
+        slopes_raw = [byte_tile("slopes_raw%d" % g, [P, 2, 2 * K_PASS]) for g in range(GROUPS)]
+        beta_sraw = byte_tile("beta_sraw", [P, S])
+        slopes_sraw = byte_tile("slopes_sraw", [P, 2, S])
+        beta_w = [byte_tile("beta_w%d" % g, [P, PACK, 2 * P]) for g in range(GROUPS)]
+        slopes_w = [byte_tile("slopes_w%d" % g, [P, 2, PACK, 2 * P]) for g in range(GROUPS)]
+        beta_s = [byte_tile("beta_s%d" % g, [P, PACK, P]) for g in range(GROUPS)]
+        slopes_s = [byte_tile("slopes_s%d" % g, [P, 2, PACK, P]) for g in range(GROUPS)]
+        hinge_w = [byte_tile("hinge_w%d" % c, [P, 2, 2 * T_CHUNK]) for c in range(CHUNKS)]
+        fourier_w = [byte_tile("fourier_w%d" % c, [P, 2 * T_CHUNK]) for c in range(CHUNKS)]
+        hinge_s = byte_tile("hinge_s", [P, 2, T])
+        fourier_s = byte_tile("fourier_s", [P, T])
+        mix_w = [keep.tile([P, N], U32, name="mix_w%d" % g, align_bytes=64) for g in range(GROUPS)]
+        mix_s = byte_tile("mix_s", [P, 2, N])
+        level_t = keep.tile([P, N], BF16, name="level_t", align_bytes=64)
+
+        def as_i32(ap):
+            return ap.bitcast(I32)
+
+        nc.vector.memset(as_i32(beta_sraw[:]), 0)
+        nc.vector.memset(as_i32(fourier_s[:]), 0)
+        nc.vector.memset(as_i32(slopes_sraw[:].rearrange("p g n -> p (g n)")), 0)
+        nc.vector.memset(as_i32(hinge_s[:].rearrange("p g n -> p (g n)")), 0)
+        nc.gpsimd.memset(as_i32(mix_s[:].rearrange("p g n -> p (g n)")), 0)
+
+        def load_scales(queue, plane, scales):
+            for q in range(4):
+                queue.dma_start(
+                    out=as_i32(plane[32 * q : 32 * q + 4]),
+                    in_=as_i32(scales[:, 4 * q : 4 * q + 4, :].rearrange("g r n -> r g n")),
+                )
+
+        def load_beta():
+            nc.sync.dma_start(out=as_i32(beta_raw[:]), in_=as_i32(beta_words[0]))
+
+        def load_slopes(g):
+            nc.sync.dma_start(
+                out=as_i32(slopes_raw[g][:]),
+                in_=as_i32(slopes_words.rearrange("k p b -> p k b")[:, :, 1024 * g : 1024 * (g + 1)]),
+            )
+
+        def load_fourier(c):
+            nc.sync.dma_start(out=as_i32(fourier_w[c][:]), in_=as_i32(fourier_words[0][:, 1024 * c : 1024 * (c + 1)]))
+
+        def load_hinge(c):
+            nc.sync.dma_start(
+                out=as_i32(hinge_w[c][:]),
+                in_=as_i32(hinge_words.rearrange("k p b -> p k b")[:, :, 1024 * c : 1024 * (c + 1)]),
+            )
+
+        def load_mix(g):
+            nc.sync.dma_start(out=as_i32(mix_w[g][:]), in_=as_i32(mix_words[g].rearrange("p n t -> p (n t)")))
+
+        beta_plane = beta_sraw[:].rearrange("p (g n) -> p g n", g=1)
+        fourier_plane = fourier_s[:].rearrange("p (g n) -> p g n", g=1)
+        load_beta()
+        load_fourier(0)
+        load_scales(nc.sync, beta_plane, beta_scales)
+        load_scales(nc.scalar, fourier_plane, fourier_scales)
+        load_scales(nc.sync, slopes_sraw, slopes_scales)
+        load_slopes(0)
+        load_scales(nc.scalar, hinge_s, hinge_scales)
+        load_hinge(0)
+        load_slopes(1)
+        load_fourier(1)
+        load_hinge(1)
+        load_mix(0)
+        load_mix(1)
+        load_scales(nc.sync, mix_s, mix_scales)
+        nc.sync.dma_start(out=level_t[:], in_=level.partition_broadcast(P))
+        for c in range(2, CHUNKS):
+            load_fourier(c)
+            load_hinge(c)
+
+        def order_beta(g):
+            cols = slice(K_PASS * g, K_PASS * (g + 1))
+            nc.vector.tensor_copy(
+                out=beta_w[g][:].rearrange("p t (m b) -> p t m b", b=2),
+                in_=beta_raw[:, 1024 * g : 1024 * (g + 1)].rearrange("p (m t b) -> p t m b", t=PACK, b=2),
+            )
+            nc.vector.tensor_copy(out=beta_s[g][:], in_=beta_sraw[:, cols].rearrange("p (m t) -> p t m", t=PACK))
+
+        def order_slopes(g, k):
+            cols = slice(K_PASS * g, K_PASS * (g + 1))
+            nc.vector.tensor_copy(
+                out=slopes_w[g][:, k].rearrange("p t (m b) -> p t m b", b=2),
+                in_=slopes_raw[g][:, k].rearrange("p (m t b) -> p t m b", t=PACK, b=2),
+            )
+            nc.vector.tensor_copy(
+                out=slopes_s[g][:, k], in_=slopes_sraw[:, k, cols].rearrange("p (m t) -> p t m", t=PACK)
+            )
+
+        season1 = {}
+        y_tiles = {}
+        codes = {}
+        out_tiles = {}
+
+        def season(c, g, t):
+            if t == 0:
+                season1[c, g] = work.tile([P, PACK, T_CHUNK], F32, name="season1", bufs=4)
+            bank = psum.tile([P, T_CHUNK], F32, name="season_bank", bufs=2)
+            nc.tensor.matmul_mx(
+                out=bank[:],
+                lhsT=beta_w[g][:, t].bitcast(FP4X4),
+                lhsT_scale=beta_s[g][:, t],
+                rhs=fourier_w[c][:].bitcast(FP4X4),
+                rhs_scale=fourier_s[:, T_CHUNK * c : T_CHUNK * (c + 1)],
+                start=True,
+                stop=True,
+            )
+            nc.scalar.activation(season1[c, g][:, t], bank[:], IDENTITY, bias=1.0)
+
+        def trend(c, g, n):
+            if g == 0:
+                y_tiles[c, n] = work.tile([P, GROUPS, T_TILE, PACK], BF16, name="y_tile", bufs=6, align_bytes=64)
+            bank = psum.tile([P, PACK, T_TILE], F32, name="trend_bank", bufs=3)
+            for t in range(PACK):
+                for k in range(2):
+                    nc.tensor.matmul_mx(
+                        out=bank[:, t],
+                        lhsT=slopes_w[g][:, k, t].bitcast(FP4X4),
+                        lhsT_scale=slopes_s[g][:, k, t],
+                        rhs=hinge_w[c][:, k, 2 * T_TILE * n : 2 * T_TILE * (n + 1)].bitcast(FP4X4),
+                        rhs_scale=hinge_s[:, k, T_CHUNK * c + T_TILE * n : T_CHUNK * c + T_TILE * (n + 1)],
+                        start=(k == 0),
+                        stop=(k == 1),
+                    )
+            nc.vector.tensor_tensor(
+                out=y_tiles[c, n][:, g].rearrange("p (c i) t -> p c t i", i=4),
+                in0=bank[:].rearrange("p t (c i) -> p c t i", i=4),
+                in1=season1[c, g][:, :, T_TILE * n : T_TILE * (n + 1)].rearrange("p t (c i) -> p c t i", i=4),
+                op=MULT,
+            )
+
+        def quantize(c, n):
+            words = work.tile([P, GROUPS, T_TILE], U32, name="y_words", bufs=5, align_bytes=64)
+            scales = work.tile([P, GROUPS, T_TILE], U8, name="y_scales", bufs=5, align_bytes=64)
+            nc.vector.quantize_mx(
+                out=words[:].rearrange("p g n -> p (g n)").bitcast(FP8X4),
+                scales=scales[:].rearrange("p g n -> p (g n)"),
+                in_=y_tiles[c, n][:].rearrange("p g n t -> p (g n t)"),
+            )
+            codes[c, n] = (words, scales)
+
+        def output(j, half):
+            c, n = divmod(j, TILES)
+            if half == 0:
+                out_tiles[j] = work.tile([P, N], F32, name="out_tile", bufs=4)
+            words, scales = codes[c, n]
+            cols = slice(512 * half, 512 * (half + 1))
+            bank = psum.tile([P, 512], F32, name="out_bank", bufs=3)
+            for g in range(GROUPS):
+                nc.tensor.matmul_mx(
+                    out=bank[:],
+                    lhsT=words[:, g].bitcast(FP8X4),
+                    lhsT_scale=scales[:, g],
+                    rhs=mix_w[g][:, cols].bitcast(FP8X4),
+                    rhs_scale=mix_s[:, g, cols],
+                    start=(g == 0),
+                    stop=(g == GROUPS - 1),
+                )
+            if half == 1 and (j % 2 == 1 or c == CHUNKS - 1) and j < 15:
+                nc.scalar.copy(out_tiles[j][:, cols], bank[:])
+                nc.gpsimd.tensor_tensor(out=out_tiles[j][:, cols], in0=out_tiles[j][:, cols], in1=level_t[:, cols], op=ADD)
+            else:
+                nc.vector.tensor_tensor(out=out_tiles[j][:, cols], in0=bank[:], in1=level_t[:, cols], op=ADD)
+            rows = slice(T_TILE * j, T_TILE * (j + 1))
+            if j == 15:
+                nc.sync.dma_start(out=out[rows, cols], in_=out_tiles[j][:, cols])
+            elif half == 1:
+                nc.sync.dma_start(out=out[rows, :], in_=out_tiles[j][:])
+
+        order_beta(0)
+        order_beta(1)
+        order_slopes(0, 0)
+        order_slopes(0, 1)
+        for t in range(PACK):
+            season(0, 0, t)
+        for t in range(PACK):
+            season(0, 1, t)
+        trend(0, 0, 0)
+        order_slopes(1, 0)
+        trend(0, 0, 1)
+        order_slopes(1, 1)
+        trend(0, 0, 2)
+        trend(0, 0, 3)
+        for j in range(CHUNKS * TILES + LAG):
+            c, n = divmod(j, TILES)
+            if 0 < c < CHUNKS:
+                trend(c, 0, n)
+            if c + 1 < CHUNKS:
+                season(c + 1, 0, n)
+            if j >= LAG:
+                output(j - LAG, 0)
+            if c < CHUNKS:
+                trend(c, 1, n)
+            if c + 1 < CHUNKS:
+                season(c + 1, 1, n)
+            if j >= LAG:
+                output(j - LAG, 1)
+            if c < CHUNKS:
+                quantize(c, n)

@@ -24,7 +24,11 @@ T_TILE = 128
 CHUNKS = T // T_CHUNK
 TILES = T_CHUNK // T_TILE
 GROUPS = S // K_PASS
-LAG = 2
+OUT_LAG = 11
+AHEAD = 4
+KINDS = "GMGMGMGM"
+G_LAG = 4
+Q_LAG = 2
 
 
 def tile_prophet_trend_seasonality_s4_kernel(
@@ -64,7 +68,6 @@ def tile_prophet_trend_seasonality_s4_kernel(
         nc.vector.memset(as_i32(fourier_s[:]), 0)
         nc.vector.memset(as_i32(slopes_sraw[:].rearrange("p g n -> p (g n)")), 0)
         nc.vector.memset(as_i32(hinge_s[:].rearrange("p g n -> p (g n)")), 0)
-        nc.gpsimd.memset(as_i32(mix_s[:].rearrange("p g n -> p (g n)")), 0)
 
         def load_scales(queue, plane, scales):
             for q in range(4):
@@ -74,7 +77,7 @@ def tile_prophet_trend_seasonality_s4_kernel(
                 )
 
         def load_beta():
-            nc.sync.dma_start(out=as_i32(beta_raw[:]), in_=as_i32(beta_words[0]))
+            nc.gpsimd.dma_start(out=as_i32(beta_raw[:]), in_=as_i32(beta_words[0]))
 
         def load_slopes(g):
             nc.sync.dma_start(
@@ -82,11 +85,11 @@ def tile_prophet_trend_seasonality_s4_kernel(
                 in_=as_i32(slopes_words.rearrange("k p b -> p k b")[:, :, 1024 * g : 1024 * (g + 1)]),
             )
 
-        def load_fourier(c):
-            nc.sync.dma_start(out=as_i32(fourier_w[c][:]), in_=as_i32(fourier_words[0][:, 1024 * c : 1024 * (c + 1)]))
+        def load_fourier(c, queue=nc.sync):
+            queue.dma_start(out=as_i32(fourier_w[c][:]), in_=as_i32(fourier_words[0][:, 1024 * c : 1024 * (c + 1)]))
 
-        def load_hinge(c):
-            nc.sync.dma_start(
+        def load_hinge(c, queue=nc.sync):
+            queue.dma_start(
                 out=as_i32(hinge_w[c][:]),
                 in_=as_i32(hinge_words.rearrange("k p b -> p k b")[:, :, 1024 * c : 1024 * (c + 1)]),
             )
@@ -97,13 +100,14 @@ def tile_prophet_trend_seasonality_s4_kernel(
         beta_plane = beta_sraw[:].rearrange("p (g n) -> p g n", g=1)
         fourier_plane = fourier_s[:].rearrange("p (g n) -> p g n", g=1)
         load_beta()
-        load_fourier(0)
+        load_fourier(0, nc.gpsimd)
+        load_hinge(0, nc.gpsimd)
+        nc.gpsimd.memset(as_i32(mix_s[:].rearrange("p g n -> p (g n)")), 0)
         load_scales(nc.sync, beta_plane, beta_scales)
-        load_scales(nc.scalar, fourier_plane, fourier_scales)
-        load_scales(nc.sync, slopes_sraw, slopes_scales)
+        load_scales(nc.sync, fourier_plane, fourier_scales)
         load_slopes(0)
-        load_scales(nc.scalar, hinge_s, hinge_scales)
-        load_hinge(0)
+        load_scales(nc.sync, slopes_sraw, slopes_scales)
+        load_scales(nc.sync, hinge_s, hinge_scales)
         load_slopes(1)
         load_fourier(1)
         load_hinge(1)
@@ -134,13 +138,18 @@ def tile_prophet_trend_seasonality_s4_kernel(
             )
 
         season1 = {}
+        trend_rows = {}
         y_tiles = {}
         codes = {}
         out_tiles = {}
+        UNITS = CHUNKS * GROUPS
+        ITEMS = UNITS * PACK
 
-        def season(c, g, t):
+        def season(k):
+            u, t = divmod(k, PACK)
+            c, g = divmod(u, GROUPS)
             if t == 0:
-                season1[c, g] = work.tile([P, PACK, T_CHUNK], F32, name="season1", bufs=4)
+                season1[u] = work.tile([P, PACK, T_CHUNK], F32, name="season1", bufs=4)
             bank = psum.tile([P, T_CHUNK], F32, name="season_bank", bufs=2)
             nc.tensor.matmul_mx(
                 out=bank[:],
@@ -151,95 +160,132 @@ def tile_prophet_trend_seasonality_s4_kernel(
                 start=True,
                 stop=True,
             )
-            nc.scalar.activation(season1[c, g][:, t], bank[:], IDENTITY, bias=1.0)
+            nc.scalar.activation(season1[u][:, t], bank[:], IDENTITY, bias=1.0)
 
-        def trend(c, g, n):
-            if g == 0:
-                y_tiles[c, n] = work.tile([P, GROUPS, T_TILE, PACK], BF16, name="y_tile", bufs=6, align_bytes=64)
-            bank = psum.tile([P, PACK, T_TILE], F32, name="trend_bank", bufs=3)
-            for t in range(PACK):
-                for k in range(2):
-                    nc.tensor.matmul_mx(
-                        out=bank[:, t],
-                        lhsT=slopes_w[g][:, k, t].bitcast(FP4X4),
-                        lhsT_scale=slopes_s[g][:, k, t],
-                        rhs=hinge_w[c][:, k, 2 * T_TILE * n : 2 * T_TILE * (n + 1)].bitcast(FP4X4),
-                        rhs_scale=hinge_s[:, k, T_CHUNK * c + T_TILE * n : T_CHUNK * c + T_TILE * (n + 1)],
-                        start=(k == 0),
-                        stop=(k == 1),
-                    )
-            nc.vector.tensor_tensor(
-                out=y_tiles[c, n][:, g].rearrange("p (c i) t -> p c t i", i=4),
-                in0=bank[:].rearrange("p t (c i) -> p c t i", i=4),
-                in1=season1[c, g][:, :, T_TILE * n : T_TILE * (n + 1)].rearrange("p t (c i) -> p c t i", i=4),
+        def piece_tile(u, i):
+            if i % 2 == 0:
+                y_tiles[u, i // 2] = work.tile([P, 2, T_TILE, PACK], BF16, name="y_tile", bufs=6, align_bytes=64)
+            return y_tiles[u, i // 2][:, i % 2]
+
+        def by_fours(ap):
+            return ap.rearrange("p t (c i) -> p c t i", i=4)
+
+        def trend_wide(k):
+            u, t = divmod(k, PACK)
+            c, g = divmod(u, GROUPS)
+            if t == 0:
+                if KINDS[u] == "G":
+                    trend_rows[u] = work.tile([P, PACK, T_CHUNK], F32, name="trend_rows", bufs=3)
+                else:
+                    trend_rows[u] = work.tile([P, PACK, T_CHUNK], BF16, name="y_rows", bufs=2)
+            bank = psum.tile([P, T_CHUNK], F32, name="trend_bank", bufs=3)
+            for j in range(2):
+                nc.tensor.matmul_mx(
+                    out=bank[:],
+                    lhsT=slopes_w[g][:, j, t].bitcast(FP4X4),
+                    lhsT_scale=slopes_s[g][:, j, t],
+                    rhs=hinge_w[c][:, j].bitcast(FP4X4),
+                    rhs_scale=hinge_s[:, j, T_CHUNK * c : T_CHUNK * (c + 1)],
+                    start=(j == 0),
+                    stop=(j == 1),
+                )
+            if KINDS[u] == "G":
+                nc.scalar.copy(trend_rows[u][:, t], bank[:])
+            else:
+                nc.vector.tensor_tensor(out=trend_rows[u][:, t], in0=bank[:], in1=season1[u][:, t], op=MULT)
+
+        def product_wide(u, i):
+            cols = slice(T_TILE * i, T_TILE * (i + 1))
+            if KINDS[u] == "B":
+                nc.scalar.copy(
+                    piece_tile(u, i).rearrange("p (c i) t -> p c t i", i=4), by_fours(trend_rows[u][:, :, cols])
+                )
+                return
+            nc.gpsimd.tensor_tensor(
+                out=piece_tile(u, i).rearrange("p (c i) t -> p c t i", i=4),
+                in0=by_fours(trend_rows[u][:, :, cols]),
+                in1=by_fours(season1[u][:, :, cols]),
                 op=MULT,
             )
 
-        def quantize(c, n):
-            words = work.tile([P, GROUPS, T_TILE], U32, name="y_words", bufs=5, align_bytes=64)
-            scales = work.tile([P, GROUPS, T_TILE], U8, name="y_scales", bufs=5, align_bytes=64)
-            nc.vector.quantize_mx(
-                out=words[:].rearrange("p g n -> p (g n)").bitcast(FP8X4),
-                scales=scales[:].rearrange("p g n -> p (g n)"),
-                in_=y_tiles[c, n][:].rearrange("p g n t -> p (g n t)"),
+        def trend_narrow(k):
+            u, n = divmod(k, PACK)
+            c, g = divmod(u, GROUPS)
+            bank = psum.tile([P, PACK, T_TILE], F32, name="trend_bank", bufs=3)
+            for t in range(PACK):
+                for j in range(2):
+                    nc.tensor.matmul_mx(
+                        out=bank[:, t],
+                        lhsT=slopes_w[g][:, j, t].bitcast(FP4X4),
+                        lhsT_scale=slopes_s[g][:, j, t],
+                        rhs=hinge_w[c][:, j, 2 * T_TILE * n : 2 * T_TILE * (n + 1)].bitcast(FP4X4),
+                        rhs_scale=hinge_s[:, j, T_CHUNK * c + T_TILE * n : T_CHUNK * c + T_TILE * (n + 1)],
+                        start=(j == 0),
+                        stop=(j == 1),
+                    )
+            nc.vector.tensor_tensor(
+                out=piece_tile(u, n).rearrange("p (c i) t -> p c t i", i=4),
+                in0=by_fours(bank[:]),
+                in1=by_fours(season1[u][:, :, T_TILE * n : T_TILE * (n + 1)]),
+                op=MULT,
             )
-            codes[c, n] = (words, scales)
 
-        def output(j, half):
+        def quantize(u, piece):
+            words = work.tile([P, 2 * T_TILE], U32, name="y_words", bufs=8, align_bytes=64)
+            scales = work.tile([P, 2 * T_TILE], U8, name="y_scales", bufs=8, align_bytes=64)
+            nc.vector.quantize_mx(
+                out=words[:].bitcast(FP8X4), scales=scales[:], in_=y_tiles[u, piece][:].rearrange("p h n t -> p (h n t)")
+            )
+            codes[u, piece] = (words, scales)
+
+        def output(h):
+            j, half = divmod(h, 2)
             c, n = divmod(j, TILES)
             if half == 0:
                 out_tiles[j] = work.tile([P, N], F32, name="out_tile", bufs=4)
-            words, scales = codes[c, n]
+            piece, i = divmod(n, 2)
+            rows = slice(T_TILE * i, T_TILE * (i + 1))
             cols = slice(512 * half, 512 * (half + 1))
             bank = psum.tile([P, 512], F32, name="out_bank", bufs=3)
             for g in range(GROUPS):
+                words, scales = codes[GROUPS * c + g, piece]
                 nc.tensor.matmul_mx(
                     out=bank[:],
-                    lhsT=words[:, g].bitcast(FP8X4),
-                    lhsT_scale=scales[:, g],
+                    lhsT=words[:, rows].bitcast(FP8X4),
+                    lhsT_scale=scales[:, rows],
                     rhs=mix_w[g][:, cols].bitcast(FP8X4),
                     rhs_scale=mix_s[:, g, cols],
                     start=(g == 0),
                     stop=(g == GROUPS - 1),
                 )
-            if half == 1 and (j % 2 == 1 or c == CHUNKS - 1) and j < 15:
-                nc.scalar.copy(out_tiles[j][:, cols], bank[:])
-                nc.gpsimd.tensor_tensor(out=out_tiles[j][:, cols], in0=out_tiles[j][:, cols], in1=level_t[:, cols], op=ADD)
-            else:
-                nc.vector.tensor_tensor(out=out_tiles[j][:, cols], in0=bank[:], in1=level_t[:, cols], op=ADD)
-            rows = slice(T_TILE * j, T_TILE * (j + 1))
-            if j == 15:
-                nc.sync.dma_start(out=out[rows, cols], in_=out_tiles[j][:, cols])
-            elif half == 1:
-                nc.sync.dma_start(out=out[rows, :], in_=out_tiles[j][:])
+            nc.vector.tensor_tensor(out=out_tiles[j][:, cols], in0=bank[:], in1=level_t[:, cols], op=ADD)
+            out_rows = slice(T_TILE * j, T_TILE * (j + 1))
+            nc.sync.dma_start(out=out[out_rows, cols], in_=out_tiles[j][:, cols])
 
         order_beta(0)
         order_beta(1)
         order_slopes(0, 0)
         order_slopes(0, 1)
-        for t in range(PACK):
-            season(0, 0, t)
-        for t in range(PACK):
-            season(0, 1, t)
-        trend(0, 0, 0)
-        order_slopes(1, 0)
-        trend(0, 0, 1)
-        order_slopes(1, 1)
-        trend(0, 0, 2)
-        trend(0, 0, 3)
-        for j in range(CHUNKS * TILES + LAG):
-            c, n = divmod(j, TILES)
-            if 0 < c < CHUNKS:
-                trend(c, 0, n)
-            if c + 1 < CHUNKS:
-                season(c + 1, 0, n)
-            if j >= LAG:
-                output(j - LAG, 0)
-            if c < CHUNKS:
-                trend(c, 1, n)
-            if c + 1 < CHUNKS:
-                season(c + 1, 1, n)
-            if j >= LAG:
-                output(j - LAG, 1)
-            if c < CHUNKS:
-                quantize(c, n)
+        for k in range(AHEAD):
+            season(k)
+        for k in range(ITEMS + OUT_LAG):
+            if k + AHEAD < ITEMS:
+                season(k + AHEAD)
+            u, t = divmod(k, PACK)
+            if k < ITEMS:
+                if KINDS[u] == "M":
+                    trend_narrow(k)
+                else:
+                    trend_wide(k)
+            if k in (0, 1):
+                order_slopes(1, k)
+            v, i = divmod(k - G_LAG, PACK)
+            if 0 <= v < UNITS and KINDS[v] != "M":
+                product_wide(v, i)
+            if k >= OUT_LAG:
+                output(k - OUT_LAG)
+            for v in range(UNITS):
+                for piece in range(2):
+                    ready = PACK * v + (2 * piece + 1 if KINDS[v] == "M" else G_LAG + Q_LAG + 2 * piece)
+                    if k == ready:
+                        quantize(v, piece)

@@ -24,11 +24,13 @@ T_TILE = 128
 CHUNKS = T // T_CHUNK
 TILES = T_CHUNK // T_TILE
 GROUPS = S // K_PASS
-OUT_LAG = 11
+OUT_LAG = 9
 AHEAD = 4
-KINDS = "GMGMGMGM"
+KINDS = "BMBMBMBM"
+OFF = set(range(1,26,4))
+OUT_RUN = 1
 G_LAG = 4
-Q_LAG = 2
+Q_LAG = 1
 
 
 def tile_prophet_trend_seasonality_s4_kernel(
@@ -55,7 +57,8 @@ def tile_prophet_trend_seasonality_s4_kernel(
         slopes_s = [byte_tile("slopes_s%d" % g, [P, 2, PACK, P]) for g in range(GROUPS)]
         hinge_w = [byte_tile("hinge_w%d" % c, [P, 2, 2 * T_CHUNK]) for c in range(CHUNKS)]
         fourier_w = [byte_tile("fourier_w%d" % c, [P, 2 * T_CHUNK]) for c in range(CHUNKS)]
-        hinge_s = byte_tile("hinge_s", [P, 2, T])
+        hinge_s0 = byte_tile("hinge_s0", [P, 2, T_CHUNK])
+        hinge_s1 = byte_tile("hinge_s1", [P, 2, T - T_CHUNK])
         fourier_s = byte_tile("fourier_s", [P, T])
         mix_w = [keep.tile([P, N], U32, name="mix_w%d" % g, align_bytes=64) for g in range(GROUPS)]
         mix_s = byte_tile("mix_s", [P, 2, N])
@@ -67,17 +70,19 @@ def tile_prophet_trend_seasonality_s4_kernel(
         nc.vector.memset(as_i32(beta_sraw[:]), 0)
         nc.vector.memset(as_i32(fourier_s[:]), 0)
         nc.vector.memset(as_i32(slopes_sraw[:].rearrange("p g n -> p (g n)")), 0)
-        nc.vector.memset(as_i32(hinge_s[:].rearrange("p g n -> p (g n)")), 0)
+        nc.vector.memset(as_i32(hinge_s0[:].rearrange("p g n -> p (g n)")), 0)
+        nc.vector.memset(as_i32(hinge_s1[:].rearrange("p g n -> p (g n)")), 0)
+        nc.vector.memset(as_i32(mix_s[:].rearrange("p g n -> p (g n)")), 0)
 
-        def load_scales(queue, plane, scales):
-            for q in range(4):
+        def load_scales(queue, plane, scales, quarters=range(4)):
+            for q in quarters:
                 queue.dma_start(
                     out=as_i32(plane[32 * q : 32 * q + 4]),
                     in_=as_i32(scales[:, 4 * q : 4 * q + 4, :].rearrange("g r n -> r g n")),
                 )
 
         def load_beta():
-            nc.gpsimd.dma_start(out=as_i32(beta_raw[:]), in_=as_i32(beta_words[0]))
+            nc.sync.dma_start(out=as_i32(beta_raw[:]), in_=as_i32(beta_words[0]))
 
         def load_slopes(g):
             nc.sync.dma_start(
@@ -99,18 +104,20 @@ def tile_prophet_trend_seasonality_s4_kernel(
 
         beta_plane = beta_sraw[:].rearrange("p (g n) -> p g n", g=1)
         fourier_plane = fourier_s[:].rearrange("p (g n) -> p g n", g=1)
-        load_beta()
-        load_fourier(0, nc.gpsimd)
-        load_hinge(0, nc.gpsimd)
-        nc.gpsimd.memset(as_i32(mix_s[:].rearrange("p g n -> p (g n)")), 0)
         load_scales(nc.sync, beta_plane, beta_scales)
-        load_scales(nc.sync, fourier_plane, fourier_scales)
-        load_slopes(0)
+        load_beta()
+        load_fourier(0)
+        load_scales(nc.sync, fourier_plane, fourier_scales, (0, 1))
+        load_scales(nc.gpsimd, fourier_plane, fourier_scales, (2, 3))
         load_scales(nc.sync, slopes_sraw, slopes_scales)
-        load_scales(nc.sync, hinge_s, hinge_scales)
+        load_slopes(0)
+        load_hinge(0)
+        load_scales(nc.gpsimd, hinge_s0, hinge_scales[:, :, 0:T_CHUNK], (0, 1))
+        load_scales(nc.sync, hinge_s0, hinge_scales[:, :, 0:T_CHUNK], (2, 3))
         load_slopes(1)
         load_fourier(1)
         load_hinge(1)
+        load_scales(nc.sync, hinge_s1, hinge_scales[:, :, T_CHUNK:T])
         load_mix(0)
         load_mix(1)
         load_scales(nc.sync, mix_s, mix_scales)
@@ -119,13 +126,16 @@ def tile_prophet_trend_seasonality_s4_kernel(
             load_fourier(c)
             load_hinge(c)
 
-        def order_beta(g):
+        def order_beta(g, first=0, last=PACK):
             cols = slice(K_PASS * g, K_PASS * (g + 1))
             nc.vector.tensor_copy(
-                out=beta_w[g][:].rearrange("p t (m b) -> p t m b", b=2),
-                in_=beta_raw[:, 1024 * g : 1024 * (g + 1)].rearrange("p (m t b) -> p t m b", t=PACK, b=2),
+                out=beta_w[g][:, first:last].rearrange("p t (m b) -> p t m b", b=2),
+                in_=beta_raw[:, 1024 * g : 1024 * (g + 1)].rearrange("p (m t b) -> p t m b", t=PACK, b=2)[:, first:last],
             )
-            nc.vector.tensor_copy(out=beta_s[g][:], in_=beta_sraw[:, cols].rearrange("p (m t) -> p t m", t=PACK))
+            nc.vector.tensor_copy(
+                out=beta_s[g][:, first:last],
+                in_=beta_sraw[:, cols].rearrange("p (m t) -> p t m", t=PACK)[:, first:last],
+            )
 
         def order_slopes(g, k):
             cols = slice(K_PASS * g, K_PASS * (g + 1))
@@ -162,6 +172,12 @@ def tile_prophet_trend_seasonality_s4_kernel(
             )
             nc.scalar.activation(season1[u][:, t], bank[:], IDENTITY, bias=1.0)
 
+        def hinge_plane(c, j, first, width):
+            if c == 0:
+                return hinge_s0[:, j, first : first + width]
+            first += T_CHUNK * (c - 1)
+            return hinge_s1[:, j, first : first + width]
+
         def piece_tile(u, i):
             if i % 2 == 0:
                 y_tiles[u, i // 2] = work.tile([P, 2, T_TILE, PACK], BF16, name="y_tile", bufs=6, align_bytes=64)
@@ -185,7 +201,7 @@ def tile_prophet_trend_seasonality_s4_kernel(
                     lhsT=slopes_w[g][:, j, t].bitcast(FP4X4),
                     lhsT_scale=slopes_s[g][:, j, t],
                     rhs=hinge_w[c][:, j].bitcast(FP4X4),
-                    rhs_scale=hinge_s[:, j, T_CHUNK * c : T_CHUNK * (c + 1)],
+                    rhs_scale=hinge_plane(c, j, 0, T_CHUNK),
                     start=(j == 0),
                     stop=(j == 1),
                 )
@@ -196,6 +212,12 @@ def tile_prophet_trend_seasonality_s4_kernel(
 
         def product_wide(u, i):
             cols = slice(T_TILE * i, T_TILE * (i + 1))
+            if KINDS[u] == "D":
+                nc.gpsimd.tensor_scalar(
+                    out=piece_tile(u, i), in0=trend_rows[u][:, :, cols].rearrange("p t n -> p n t"),
+                    scalar1=1.0, scalar2=0.0, op0=MULT, op1=ADD,
+                )
+                return
             if KINDS[u] == "B":
                 nc.scalar.copy(
                     piece_tile(u, i).rearrange("p (c i) t -> p c t i", i=4), by_fours(trend_rows[u][:, :, cols])
@@ -219,7 +241,7 @@ def tile_prophet_trend_seasonality_s4_kernel(
                         lhsT=slopes_w[g][:, j, t].bitcast(FP4X4),
                         lhsT_scale=slopes_s[g][:, j, t],
                         rhs=hinge_w[c][:, j, 2 * T_TILE * n : 2 * T_TILE * (n + 1)].bitcast(FP4X4),
-                        rhs_scale=hinge_s[:, j, T_CHUNK * c + T_TILE * n : T_CHUNK * c + T_TILE * (n + 1)],
+                        rhs_scale=hinge_plane(c, j, T_TILE * n, T_TILE),
                         start=(j == 0),
                         stop=(j == 1),
                     )
@@ -242,7 +264,7 @@ def tile_prophet_trend_seasonality_s4_kernel(
             j, half = divmod(h, 2)
             c, n = divmod(j, TILES)
             if half == 0:
-                out_tiles[j] = work.tile([P, N], F32, name="out_tile", bufs=4)
+                out_tiles[j] = work.tile([P, N], F32, name="out_tile", bufs=8)
             piece, i = divmod(n, 2)
             rows = slice(T_TILE * i, T_TILE * (i + 1))
             cols = slice(512 * half, 512 * (half + 1))
@@ -258,11 +280,16 @@ def tile_prophet_trend_seasonality_s4_kernel(
                     start=(g == 0),
                     stop=(g == GROUPS - 1),
                 )
-            nc.vector.tensor_tensor(out=out_tiles[j][:, cols], in0=bank[:], in1=level_t[:, cols], op=ADD)
+            if h in OFF:
+                nc.scalar.copy(out_tiles[j][:, cols], bank[:])
+                nc.gpsimd.tensor_tensor(out=out_tiles[j][:, cols], in0=out_tiles[j][:, cols], in1=level_t[:, cols], op=ADD)
+            else:
+                nc.vector.tensor_tensor(out=out_tiles[j][:, cols], in0=bank[:], in1=level_t[:, cols], op=ADD)
             out_rows = slice(T_TILE * j, T_TILE * (j + 1))
             nc.sync.dma_start(out=out[out_rows, cols], in_=out_tiles[j][:, cols])
 
-        order_beta(0)
+        order_beta(0, 0, 1)
+        order_beta(0, 1, PACK)
         order_beta(1)
         order_slopes(0, 0)
         order_slopes(0, 1)
@@ -282,8 +309,10 @@ def tile_prophet_trend_seasonality_s4_kernel(
             v, i = divmod(k - G_LAG, PACK)
             if 0 <= v < UNITS and KINDS[v] != "M":
                 product_wide(v, i)
-            if k >= OUT_LAG:
-                output(k - OUT_LAG)
+            h = k - OUT_LAG
+            if h >= 0 and h % OUT_RUN == 0:
+                for i in range(min(OUT_RUN, 32 - h)):
+                    output(h + i)
             for v in range(UNITS):
                 for piece in range(2):
                     ready = PACK * v + (2 * piece + 1 if KINDS[v] == "M" else G_LAG + Q_LAG + 2 * piece)

@@ -24,10 +24,10 @@ T_TILE = 128
 CHUNKS = T // T_CHUNK
 TILES = T_CHUNK // T_TILE
 GROUPS = S // K_PASS
-OUT_LAG = 9
-AHEAD = 4
-KINDS = "BMBMBMBM"
-OFF = set(range(1,26,4))
+OUT_LAG = 11
+AHEAD = 3
+KINDS = "DBDBDBBM"
+OFF = set()
 OUT_RUN = 1
 G_LAG = 4
 Q_LAG = 1
@@ -104,16 +104,14 @@ def tile_prophet_trend_seasonality_s4_kernel(
 
         beta_plane = beta_sraw[:].rearrange("p (g n) -> p g n", g=1)
         fourier_plane = fourier_s[:].rearrange("p (g n) -> p g n", g=1)
-        load_scales(nc.sync, beta_plane, beta_scales)
         load_beta()
+        load_scales(nc.sync, beta_plane, beta_scales)
         load_fourier(0)
-        load_scales(nc.sync, fourier_plane, fourier_scales, (0, 1))
-        load_scales(nc.gpsimd, fourier_plane, fourier_scales, (2, 3))
+        load_scales(nc.sync, fourier_plane, fourier_scales)
         load_scales(nc.sync, slopes_sraw, slopes_scales)
         load_slopes(0)
         load_hinge(0)
-        load_scales(nc.gpsimd, hinge_s0, hinge_scales[:, :, 0:T_CHUNK], (0, 1))
-        load_scales(nc.sync, hinge_s0, hinge_scales[:, :, 0:T_CHUNK], (2, 3))
+        load_scales(nc.sync, hinge_s0, hinge_scales[:, :, 0:T_CHUNK])
         load_slopes(1)
         load_fourier(1)
         load_hinge(1)
@@ -191,7 +189,7 @@ def tile_prophet_trend_seasonality_s4_kernel(
             c, g = divmod(u, GROUPS)
             if t == 0:
                 if KINDS[u] == "G":
-                    trend_rows[u] = work.tile([P, PACK, T_CHUNK], F32, name="trend_rows", bufs=3)
+                    trend_rows[u] = work.tile([P, PACK, T_CHUNK], F32, name="trend_rows", bufs=2)
                 else:
                     trend_rows[u] = work.tile([P, PACK, T_CHUNK], BF16, name="y_rows", bufs=2)
             bank = psum.tile([P, T_CHUNK], F32, name="trend_bank", bufs=3)
@@ -267,12 +265,20 @@ def tile_prophet_trend_seasonality_s4_kernel(
                 out_tiles[j] = work.tile([P, N], F32, name="out_tile", bufs=8)
             piece, i = divmod(n, 2)
             rows = slice(T_TILE * i, T_TILE * (i + 1))
-            cols = slice(512 * half, 512 * (half + 1))
+            pieces = 2 if h == 31 else 1
+            width = 512 // pieces
+            for first in range(512 * half, 512 * (half + 1), width):
+                output_piece(h, rows, slice(first, first + width), piece)
+
+        def output_piece(h, rows, cols, piece):
+            j = h // 2
+            c = j // TILES
+            width = cols.stop - cols.start
             bank = psum.tile([P, 512], F32, name="out_bank", bufs=3)
             for g in range(GROUPS):
                 words, scales = codes[GROUPS * c + g, piece]
                 nc.tensor.matmul_mx(
-                    out=bank[:],
+                    out=bank[:, :width],
                     lhsT=words[:, rows].bitcast(FP8X4),
                     lhsT_scale=scales[:, rows],
                     rhs=mix_w[g][:, cols].bitcast(FP8X4),
@@ -281,12 +287,11 @@ def tile_prophet_trend_seasonality_s4_kernel(
                     stop=(g == GROUPS - 1),
                 )
             if h in OFF:
-                nc.scalar.copy(out_tiles[j][:, cols], bank[:])
+                nc.scalar.copy(out_tiles[j][:, cols], bank[:, :width])
                 nc.gpsimd.tensor_tensor(out=out_tiles[j][:, cols], in0=out_tiles[j][:, cols], in1=level_t[:, cols], op=ADD)
             else:
-                nc.vector.tensor_tensor(out=out_tiles[j][:, cols], in0=bank[:], in1=level_t[:, cols], op=ADD)
-            out_rows = slice(T_TILE * j, T_TILE * (j + 1))
-            nc.sync.dma_start(out=out[out_rows, cols], in_=out_tiles[j][:, cols])
+                nc.vector.tensor_tensor(out=out_tiles[j][:, cols], in0=bank[:, :width], in1=level_t[:, cols], op=ADD)
+            nc.sync.dma_start(out=out[T_TILE * j : T_TILE * (j + 1), cols], in_=out_tiles[j][:, cols])
 
         order_beta(0, 0, 1)
         order_beta(0, 1, PACK)

from contextlib import ExitStack

import concourse.mybir as mybir

T, C, F, S, N = 2048, 1024, 512, 1024, 1024
FLOPS = 2 * T * S * (C + F) + 2 * T * S * N

F32 = mybir.dt.float32
BF16 = mybir.dt.bfloat16
I32 = mybir.dt.int32
U32 = mybir.dt.uint32
U8 = mybir.dt.uint8
FP4X4 = mybir.dt.float4_e2m1fn_x4
FP8X4 = mybir.dt.float8_e4m3fn_x4
ADD = mybir.AluOpType.add
MULT = mybir.AluOpType.mult
IDENTITY = mybir.ActivationFunctionType.Identity

P = 128
PACK = 4
K_PASS = P * PACK
T_CHUNK = 512
T_TILE = 128
CHUNKS = T // T_CHUNK
TILES = T_CHUNK // T_TILE
GROUPS = S // K_PASS
OUT_LAG = 11
AHEAD = 3
KINDS = "DBDBDBBM"
OFF = set()
OUT_RUN = 1
G_LAG = 4
Q_LAG = 1


def tile_prophet_trend_seasonality_s4_kernel(
    tc, hinge_words, hinge_scales, slopes_words, slopes_scales, fourier_words, fourier_scales,
    beta_words, beta_scales, mix_words, mix_scales, level, out,
):
    nc = tc.nc
    with ExitStack() as ctx:
        ctx.enter_context(tc.manual_schedule())
        keep = ctx.enter_context(tc.tile_pool(name="keep", bufs=1))
        work = ctx.enter_context(tc.tile_pool(name="work", bufs=4))
        psum = ctx.enter_context(tc.psum_pool(name="psum", bufs=2))

        def byte_tile(label, shape):
            return keep.tile(shape, U8, name=label, align_bytes=64)

        beta_raw = byte_tile("beta_raw", [P, 2 * S])
        slopes_raw = [byte_tile("slopes_raw%d" % g, [P, 2, 2 * K_PASS]) for g in range(GROUPS)]
        beta_sraw = byte_tile("beta_sraw", [P, S])
        slopes_sraw = byte_tile("slopes_sraw", [P, 2, S])
        beta_w = [byte_tile("beta_w%d" % g, [P, PACK, 2 * P]) for g in range(GROUPS)]
        slopes_w = [byte_tile("slopes_w%d" % g, [P, 2, PACK, 2 * P]) for g in range(GROUPS)]
        beta_s = [byte_tile("beta_s%d" % g, [P, PACK, P]) for g in range(GROUPS)]
        slopes_s = [byte_tile("slopes_s%d" % g, [P, 2, PACK, P]) for g in range(GROUPS)]
        hinge_w = [byte_tile("hinge_w%d" % c, [P, 2, 2 * T_CHUNK]) for c in range(CHUNKS)]
        fourier_w = [byte_tile("fourier_w%d" % c, [P, 2 * T_CHUNK]) for c in range(CHUNKS)]
        hinge_s0 = byte_tile("hinge_s0", [P, 2, T_CHUNK])
        hinge_s1 = byte_tile("hinge_s1", [P, 2, T - T_CHUNK])
        fourier_s = byte_tile("fourier_s", [P, T])
        mix_w = [keep.tile([P, N], U32, name="mix_w%d" % g, align_bytes=64) for g in range(GROUPS)]
        mix_s = byte_tile("mix_s", [P, 2, N])
        level_t = keep.tile([P, N], BF16, name="level_t", align_bytes=64)

        def as_i32(ap):
            return ap.bitcast(I32)

        nc.vector.memset(as_i32(beta_sraw[:]), 0)
        nc.vector.memset(as_i32(fourier_s[:]), 0)
        nc.vector.memset(as_i32(slopes_sraw[:].rearrange("p g n -> p (g n)")), 0)
        nc.vector.memset(as_i32(hinge_s0[:].rearrange("p g n -> p (g n)")), 0)
        nc.vector.memset(as_i32(hinge_s1[:].rearrange("p g n -> p (g n)")), 0)
        nc.vector.memset(as_i32(mix_s[:].rearrange("p g n -> p (g n)")), 0)

        def load_scales(queue, plane, scales, quarters=range(4)):
            for q in quarters:
                queue.dma_start(
                    out=as_i32(plane[32 * q : 32 * q + 4]),
                    in_=as_i32(scales[:, 4 * q : 4 * q + 4, :].rearrange("g r n -> r g n")),
                )

        def load_beta():
            nc.sync.dma_start(out=as_i32(beta_raw[:]), in_=as_i32(beta_words[0]))

        def load_slopes(g):
            nc.sync.dma_start(
                out=as_i32(slopes_raw[g][:]),
                in_=as_i32(slopes_words.rearrange("k p b -> p k b")[:, :, 1024 * g : 1024 * (g + 1)]),
            )

        def load_fourier(c, queue=nc.sync):
            queue.dma_start(out=as_i32(fourier_w[c][:]), in_=as_i32(fourier_words[0][:, 1024 * c : 1024 * (c + 1)]))

        def load_hinge(c, queue=nc.sync):
            queue.dma_start(
                out=as_i32(hinge_w[c][:]),
                in_=as_i32(hinge_words.rearrange("k p b -> p k b")[:, :, 1024 * c : 1024 * (c + 1)]),
            )

        def load_mix(g):
            nc.sync.dma_start(out=as_i32(mix_w[g][:]), in_=as_i32(mix_words[g].rearrange("p n t -> p (n t)")))

        beta_plane = beta_sraw[:].rearrange("p (g n) -> p g n", g=1)
        fourier_plane = fourier_s[:].rearrange("p (g n) -> p g n", g=1)
        load_beta()
        load_scales(nc.sync, beta_plane, beta_scales)
        load_fourier(0)
        load_scales(nc.sync, fourier_plane, fourier_scales)
        load_scales(nc.sync, slopes_sraw, slopes_scales)
        load_slopes(0)
        load_hinge(0)
        load_scales(nc.sync, hinge_s0, hinge_scales[:, :, 0:T_CHUNK])
        load_slopes(1)
        load_fourier(1)
        load_hinge(1)
        load_scales(nc.sync, hinge_s1, hinge_scales[:, :, T_CHUNK:T])
        load_mix(0)
        load_mix(1)
        load_scales(nc.sync, mix_s, mix_scales)
        nc.sync.dma_start(out=level_t[:], in_=level.partition_broadcast(P))
        for c in range(2, CHUNKS):
            load_fourier(c)
            load_hinge(c)

        def order_beta(g, first=0, last=PACK):
            cols = slice(K_PASS * g, K_PASS * (g + 1))
            nc.vector.tensor_copy(
                out=beta_w[g][:, first:last].rearrange("p t (m b) -> p t m b", b=2),
                in_=beta_raw[:, 1024 * g : 1024 * (g + 1)].rearrange("p (m t b) -> p t m b", t=PACK, b=2)[:, first:last],
            )
            nc.vector.tensor_copy(
                out=beta_s[g][:, first:last],
                in_=beta_sraw[:, cols].rearrange("p (m t) -> p t m", t=PACK)[:, first:last],
            )

        def order_slopes(g, k):
            cols = slice(K_PASS * g, K_PASS * (g + 1))
            nc.vector.tensor_copy(
                out=slopes_w[g][:, k].rearrange("p t (m b) -> p t m b", b=2),
                in_=slopes_raw[g][:, k].rearrange("p (m t b) -> p t m b", t=PACK, b=2),
            )
            nc.vector.tensor_copy(
                out=slopes_s[g][:, k], in_=slopes_sraw[:, k, cols].rearrange("p (m t) -> p t m", t=PACK)
            )

        season1 = {}
        trend_rows = {}
        y_tiles = {}
        codes = {}
        out_tiles = {}
        UNITS = CHUNKS * GROUPS
        ITEMS = UNITS * PACK

        def season(k):
            u, t = divmod(k, PACK)
            c, g = divmod(u, GROUPS)
            if t == 0:
                season1[u] = work.tile([P, PACK, T_CHUNK], F32, name="season1", bufs=4)
            bank = psum.tile([P, T_CHUNK], F32, name="season_bank", bufs=2)
            nc.tensor.matmul_mx(
                out=bank[:],
                lhsT=beta_w[g][:, t].bitcast(FP4X4),
                lhsT_scale=beta_s[g][:, t],
                rhs=fourier_w[c][:].bitcast(FP4X4),
                rhs_scale=fourier_s[:, T_CHUNK * c : T_CHUNK * (c + 1)],
                start=True,
                stop=True,
            )
            nc.scalar.activation(season1[u][:, t], bank[:], IDENTITY, bias=1.0)

        def hinge_plane(c, j, first, width):
            if c == 0:
                return hinge_s0[:, j, first : first + width]
            first += T_CHUNK * (c - 1)
            return hinge_s1[:, j, first : first + width]

        def piece_tile(u, i):
            if i % 2 == 0:
                y_tiles[u, i // 2] = work.tile([P, 2, T_TILE, PACK], BF16, name="y_tile", bufs=6, align_bytes=64)
            return y_tiles[u, i // 2][:, i % 2]

        def by_fours(ap):
            return ap.rearrange("p t (c i) -> p c t i", i=4)

        def trend_wide(k):
            u, t = divmod(k, PACK)
            c, g = divmod(u, GROUPS)
            if t == 0:
                if KINDS[u] == "G":
                    trend_rows[u] = work.tile([P, PACK, T_CHUNK], F32, name="trend_rows", bufs=2)
                else:
                    trend_rows[u] = work.tile([P, PACK, T_CHUNK], BF16, name="y_rows", bufs=2)
            bank = psum.tile([P, T_CHUNK], F32, name="trend_bank", bufs=3)
            for j in range(2):
                nc.tensor.matmul_mx(
                    out=bank[:],
                    lhsT=slopes_w[g][:, j, t].bitcast(FP4X4),
                    lhsT_scale=slopes_s[g][:, j, t],
                    rhs=hinge_w[c][:, j].bitcast(FP4X4),
                    rhs_scale=hinge_plane(c, j, 0, T_CHUNK),
                    start=(j == 0),
                    stop=(j == 1),
                )
            if KINDS[u] == "G":
                nc.scalar.copy(trend_rows[u][:, t], bank[:])
            else:
                nc.vector.tensor_tensor(out=trend_rows[u][:, t], in0=bank[:], in1=season1[u][:, t], op=MULT)

        def product_wide(u, i):
            cols = slice(T_TILE * i, T_TILE * (i + 1))
            if KINDS[u] == "D":
                nc.gpsimd.tensor_scalar(
                    out=piece_tile(u, i), in0=trend_rows[u][:, :, cols].rearrange("p t n -> p n t"),
                    scalar1=1.0, scalar2=0.0, op0=MULT, op1=ADD,
                )
                return
            if KINDS[u] == "B":
                nc.scalar.copy(
                    piece_tile(u, i).rearrange("p (c i) t -> p c t i", i=4), by_fours(trend_rows[u][:, :, cols])
                )
                return
            nc.gpsimd.tensor_tensor(
                out=piece_tile(u, i).rearrange("p (c i) t -> p c t i", i=4),
                in0=by_fours(trend_rows[u][:, :, cols]),
                in1=by_fours(season1[u][:, :, cols]),
                op=MULT,
            )

        def trend_narrow(k):
            u, n = divmod(k, PACK)
            c, g = divmod(u, GROUPS)
            bank = psum.tile([P, PACK, T_TILE], F32, name="trend_bank", bufs=3)
            for t in range(PACK):
                for j in range(2):
                    nc.tensor.matmul_mx(
                        out=bank[:, t],
                        lhsT=slopes_w[g][:, j, t].bitcast(FP4X4),
                        lhsT_scale=slopes_s[g][:, j, t],
                        rhs=hinge_w[c][:, j, 2 * T_TILE * n : 2 * T_TILE * (n + 1)].bitcast(FP4X4),
                        rhs_scale=hinge_plane(c, j, T_TILE * n, T_TILE),
                        start=(j == 0),
                        stop=(j == 1),
                    )
            nc.vector.tensor_tensor(
                out=piece_tile(u, n).rearrange("p (c i) t -> p c t i", i=4),
                in0=by_fours(bank[:]),
                in1=by_fours(season1[u][:, :, T_TILE * n : T_TILE * (n + 1)]),
                op=MULT,
            )

        def quantize(u, piece):
            words = work.tile([P, 2 * T_TILE], U32, name="y_words", bufs=8, align_bytes=64)
            scales = work.tile([P, 2 * T_TILE], U8, name="y_scales", bufs=8, align_bytes=64)
            nc.vector.quantize_mx(
                out=words[:].bitcast(FP8X4), scales=scales[:], in_=y_tiles[u, piece][:].rearrange("p h n t -> p (h n t)")
            )
            codes[u, piece] = (words, scales)

        def output(h):
            j, half = divmod(h, 2)
            c, n = divmod(j, TILES)
            if half == 0:
                out_tiles[j] = work.tile([P, N], F32, name="out_tile", bufs=8)
            piece, i = divmod(n, 2)
            rows = slice(T_TILE * i, T_TILE * (i + 1))
            pieces = 2 if h == 31 else 1
            width = 512 // pieces
            for first in range(512 * half, 512 * (half + 1), width):
                output_piece(h, rows, slice(first, first + width), piece)

        def output_piece(h, rows, cols, piece):
            j = h // 2
            c = j // TILES
            width = cols.stop - cols.start
            bank = psum.tile([P, 512], F32, name="out_bank", bufs=3)
            for g in range(GROUPS):
                words, scales = codes[GROUPS * c + g, piece]
                nc.tensor.matmul_mx(
                    out=bank[:, :width],
                    lhsT=words[:, rows].bitcast(FP8X4),
                    lhsT_scale=scales[:, rows],
                    rhs=mix_w[g][:, cols].bitcast(FP8X4),
                    rhs_scale=mix_s[:, g, cols],
                    start=(g == 0),
                    stop=(g == GROUPS - 1),
                )
            if h in OFF:
                nc.scalar.copy(out_tiles[j][:, cols], bank[:, :width])
                nc.gpsimd.tensor_tensor(out=out_tiles[j][:, cols], in0=out_tiles[j][:, cols], in1=level_t[:, cols], op=ADD)
            else:
                nc.vector.tensor_tensor(out=out_tiles[j][:, cols], in0=bank[:, :width], in1=level_t[:, cols], op=ADD)
            nc.sync.dma_start(out=out[T_TILE * j : T_TILE * (j + 1), cols], in_=out_tiles[j][:, cols])

        order_beta(0, 0, 1)
        order_beta(0, 1, PACK)
        order_beta(1)
        order_slopes(0, 0)
        order_slopes(0, 1)
        for k in range(AHEAD):
            season(k)
        for k in range(ITEMS + OUT_LAG):
            if k + AHEAD < ITEMS:
                season(k + AHEAD)
            u, t = divmod(k, PACK)
            if k < ITEMS:
                if KINDS[u] == "M":
                    trend_narrow(k)
                else:
                    trend_wide(k)
            if k in (0, 1):
                order_slopes(1, k)
            v, i = divmod(k - G_LAG, PACK)
            if 0 <= v < UNITS and KINDS[v] != "M":
                product_wide(v, i)
            h = k - OUT_LAG
            if h >= 0 and h % OUT_RUN == 0:
                for i in range(min(OUT_RUN, 32 - h)):
                    output(h + i)
            for v in range(UNITS):
                for piece in range(2):
                    ready = PACK * v + (2 * piece + 1 if KINDS[v] == "M" else G_LAG + Q_LAG + 2 * piece)
                    if k == ready:
                        quantize(v, piece)
